import numpy as np
import ml_dtypes


def mxq(x, axis, fmt="e4m3"):
    dtype, down = {"e4m3": (ml_dtypes.float8_e4m3fn, 7), "e5m2": (ml_dtypes.float8_e5m2, 14)}[fmt]
    v = np.moveaxis(np.asarray(x, np.float32).astype(ml_dtypes.bfloat16).astype(np.float64), axis, -1)
    blocks = v.reshape(v.shape[:-1] + (-1, 32))
    amax = np.abs(blocks).max(-1, keepdims=True)
    byte = np.maximum(np.where(amax > 0, np.frexp(amax)[1] - 1 + 127, 0) - down, 1)
    scale = np.exp2(byte - 127.0)
    codes = (blocks / scale).astype(np.float32).astype(dtype).astype(np.float64)
    return np.moveaxis((codes * scale).reshape(v.shape), -1, axis)


WIDE = False


def mx_kscale(k):
    if not WIDE:
        return np.ones(k)
    levels = np.array([10, -10, 5, -5, 0])
    if k % 512:
        return np.exp2(np.random.permutation(np.resize(levels, k // 32))).repeat(32)
    a = np.empty((k // 512, 16))
    for p in range(k // 512):
        a[p, :8] = np.random.permutation(np.resize(levels, 8))
        for g in range(8):
            far = levels[np.abs(levels - a[p, g]) >= 10]
            a[p, g + 8] = far[np.random.randint(len(far))]
    return np.exp2(a.ravel()).repeat(32)


BF16 = ml_dtypes.bfloat16


def bf(x):
    return np.asarray(x, np.float32).astype(BF16)


def f64(x):
    return np.asarray(x).astype(np.float64)

def planes(Y):
    n, m = Y.shape
    b = f64(bf(Y)).reshape(n // 32, 32, m)
    amax = np.abs(b).max(1)
    byte = np.clip(np.where(amax > 0, np.frexp(amax)[1] - 1 + 127 - 7, 1), 1, 254)
    codes = (b * np.exp2(127.0 - byte)[:, None, :]).reshape(n, m).astype(np.float32).astype(ml_dtypes.float8_e4m3fn).view(np.uint8)
    words = codes.reshape(n // 512, 128, 4, m).transpose(0, 1, 3, 2)
    return np.ascontiguousarray(words), np.ascontiguousarray(byte.astype(np.uint8).reshape(n // 512, 16, m))


Q, B, N, D, E, K = 512, 128, 16, 512, 512, 6
N1 = N + 1


def setup_inputs():
    s = mx_kscale(D)
    t = mx_kscale(E)
    q = 1.4 * np.random.standard_normal((Q, E)) / np.sqrt(E) / t
    topic = 0.8 * np.random.standard_normal((B, 1, D))
    x = (topic + 0.6 * np.random.standard_normal((B, N1, D))) * s
    w = np.random.standard_normal((2, D, E)) / np.sqrt(2 * D) / s[None, :, None]
    bias = 0.3 * np.random.standard_normal(E)
    gain = np.random.standard_normal(E) * t
    mu = np.random.uniform(-1.5, 1.5, K)
    sigma = np.random.uniform(0.5, 0.9, K)
    return {"q": bf(q), "x": bf(x), "w": bf(w), "bias": bf(bias), "gain": bf(gain), "mu": bf(mu), "sigma": bf(sigma)}


def bigram_features(x, w, bias, gain):
    xq = mxq(f64(x), 2, "e4m3")
    wq = mxq(f64(w), 1, "e4m3")
    xa = xq[:, 0:N, :].reshape(B * N, D)
    xb = xq[:, 1:N + 1, :].reshape(B * N, D)
    h = (xa @ wq[0]) + (xb @ wq[1]) + f64(bias)
    return np.maximum(h, 0.0) * f64(gain)


def log_mean_exp_over_n(z):
    n = z.shape[2]
    m = np.max(z, axis=2, keepdims=True)
    total = np.sum(np.exp(z - m), axis=2)
    lse = np.log(total) + np.squeeze(m, axis=2)
    return lse - np.log(n)


def core(q, x, w, bias, gain, mu, sigma):
    d = bigram_features(x, w, bias, gain)
    sc = (mxq(f64(q), 1, "e4m3") @ mxq(d, 1, "e4m3").T).reshape(Q, B, N)
    diff = sc[:, :, :, None] - f64(mu)
    sg = f64(sigma)
    z = -(diff * diff) / (2.0 * (sg * sg))
    return log_mean_exp_over_n(z)


def reference(q, x, w, bias, gain, mu, sigma):
    R_out = core(q, x, w, bias, gain, mu, sigma)
    words, scales = planes(np.moveaxis(R_out, 0, 0).reshape(512, -1))
    return R_out, words, scales

@@ -1,0 +1,296 @@
+from contextlib import ExitStack
+
+import concourse.mybir as mybir
+from concourse.masks import make_identity
+
+Q, B, N, D, E, K = 512, 128, 16, 512, 512, 6
+FLOPS = 2 * (2 * B * N * D * E + Q * B * N * E)
+
+F32 = mybir.dt.float32
+BF16 = mybir.dt.bfloat16
+U32 = mybir.dt.uint32
+I32 = mybir.dt.int32
+U8 = mybir.dt.uint8
+FP8X4 = mybir.dt.float8_e4m3fn_x4
+ACT = mybir.ActivationFunctionType
+ALU = mybir.AluOpType
+AX = mybir.AxisListType
+ENG = mybir.EngineType
+
+P = 128
+T = 4
+BLK = 512
+NB = 4
+
+
+def tile_bigramconvkernelpoolingmatch_x1_kernel(tc, q, x, w, bias, gain, mu, sigma, out_0, out_1, out_2):
+    nc = tc.nc
+    with ExitStack() as ctx:
+        keep = ctx.enter_context(tc.tile_pool(name="keep", bufs=1))
+        work = ctx.enter_context(tc.tile_pool(name="work", bufs=2))
+        ypool = ctx.enter_context(tc.tile_pool(name="ypool", bufs=5))
+        epool = ctx.enter_context(tc.tile_pool(name="epool", bufs=8))
+        spsum = ctx.enter_context(tc.psum_pool(name="spsum", bufs=4))
+        xpsum = ctx.enter_context(tc.psum_pool(name="xpsum", bufs=3))
+        upsum = ctx.enter_context(tc.psum_pool(name="upsum", bufs=1))
+
+        x_groups = [(0, 1), (1, 5), (5, 9), (9, 13), (13, 17)]
+        x_raw = []
+        for g, (n0, n1) in enumerate(x_groups):
+            x_raw.append(keep.tile([P, (n1 - n0) * D], BF16, name="x_raw%d" % g))
+        w_raw = []
+        for s in range(2):
+            w_raw.append(keep.tile([P, 4, E], BF16, name="w_raw%d" % s))
+        q_raw = keep.tile([P, T * E], BF16, name="q_raw")
+
+        def load_x(g):
+            n0, n1 = x_groups[g]
+            nc.sync.dma_start(out=x_raw[g][:], in_=x[:, n0:n1, :].rearrange("b n d -> b (n d)"))
+
+        gain_sb = keep.tile([P, 4], BF16, name="gain_sb")
+        bias_sb = keep.tile([P, 4], BF16, name="bias_sb")
+        mu_sb = keep.tile([P, K], BF16, name="mu_sb")
+        sigma_sb = keep.tile([P, K], BF16, name="sigma_sb")
+
+        load_x(0)
+        load_x(1)
+        nc.sync.dma_start(out=w_raw[0][:], in_=w[0].rearrange("(p j) c -> p j c", j=4))
+        nc.sync.dma_start(out=w_raw[1][:], in_=w[1].rearrange("(p j) c -> p j c", j=4))
+        nc.scalar.dma_start(out=gain_sb[:], in_=gain.rearrange("(p t) -> p t", t=4))
+        nc.scalar.dma_start(out=bias_sb[:], in_=bias.rearrange("(p t) -> p t", t=4))
+        nc.scalar.dma_start(out=mu_sb[:], in_=mu.partition_broadcast(P))
+        nc.scalar.dma_start(out=sigma_sb[:], in_=sigma.partition_broadcast(P))
+        load_x(2)
+        nc.sync.dma_start(out=q_raw[:], in_=q.rearrange("(m t) k -> m (t k)", t=T))
+        load_x(3)
+        load_x(4)
+
+        ident = keep.tile([P, P], F32, name="ident")
+        make_identity(nc, ident[:])
+
+        gain_abs = keep.tile([P, 4], F32, name="gain_abs")
+        gain_bias = keep.tile([P, 4], F32, name="gain_bias")
+        sign01 = keep.tile([P, 4], F32, name="sign01")
+        sign = keep.tile([P, 4], BF16, name="sign")
+        nc.scalar.activation(out=gain_abs[:], in_=gain_sb[:], func=ACT.Abs)
+        nc.vector.tensor_tensor(out=gain_bias[:], in0=gain_abs[:], in1=bias_sb[:], op=ALU.mult)
+        nc.vector.tensor_scalar(out=sign01[:], in0=gain_sb[:], scalar1=0.0, scalar2=2.0, op0=ALU.is_ge, op1=ALU.mult)
+        nc.vector.tensor_scalar(out=sign[:], in0=sign01[:], scalar1=1.0, scalar2=None, op0=ALU.subtract)
+        z_scale = keep.tile([P, K], F32, name="z_scale")
+        z_bias = keep.tile([P, K], F32, name="z_bias")
+        rsig = keep.tile([P, K], F32, name="rsig")
+        nc.vector.reciprocal(out=rsig[:], in_=sigma_sb[:])
+        nc.vector.tensor_scalar(out=z_scale[:], in0=rsig[:], scalar1=0.7071067811865476, scalar2=None, op0=ALU.mult)
+        nc.vector.scalar_tensor_tensor(out=z_bias[:], in0=mu_sb[:], scalar=-1.0, in1=z_scale[:], op0=ALU.mult, op1=ALU.mult)
+
+        w_codes = []
+        w_scales = []
+        for s in range(2):
+            w_codes.append(keep.tile([P, E], U32, align_bytes=64, name="w_codes%d" % s))
+            w_scales.append(keep.tile([P, E], U8, align_bytes=64, name="w_scales%d" % s))
+        x_codes = keep.tile([P, (N + 1) * B], U32, align_bytes=64, name="x_codes")
+        x_scales = keep.tile([P, (N + 1) * B], U8, align_bytes=64, name="x_scales")
+        q_codes = keep.tile([P, Q], U32, align_bytes=64, name="q_codes")
+        q_scales = keep.tile([P, Q], U8, align_bytes=64, name="q_scales")
+        d_codes = keep.tile([P, N * B], U32, align_bytes=64, name="d_codes")
+        d_scales = keep.tile([P, N * B], U8, align_bytes=64, name="d_scales")
+
+        def transpose_words(raw, slot, bank, place):
+            words = raw[:, slot * D : (slot + 1) * D].bitcast(F32)
+            for u in range(2):
+                nc.tensor.transpose(bank[:, place, u, :], words[:, u : D // 2 : 2], ident[:])
+
+        def turn_pair(raw, slots, grouped, first_col):
+            bank = xpsum.tile([P, 2, 2, P], F32, name="x_bank", tag="xb")
+            for place, slot in enumerate(slots):
+                transpose_words(raw, slot, bank, place)
+            n = len(slots)
+            cols = slice(first_col * 4, (first_col + n * P) * 4)
+            nc.scalar.copy(
+                out=grouped[:, cols].bitcast(F32).rearrange("p (n r u) -> p n r u", n=n, u=2),
+                in_=bank[:, 0:n].rearrange("p n u r -> p n r u"),
+            )
+
+        def prepare_w(s):
+            grouped = work.tile([P, 4 * E], BF16, align_bytes=64, name="w_grouped", tag="wg")
+            nc.vector.tensor_copy(
+                out=grouped[:].rearrange("p (t m j) -> p t m j", t=4, j=4),
+                in_=w_raw[s][:].rearrange("p j (m t) -> p t m j", t=4),
+            )
+            nc.vector.quantize_mx(out=w_codes[s][:].bitcast(FP8X4), scales=w_scales[s][:], in_=grouped[:])
+
+        def prepare_x(g):
+            n0, n1 = x_groups[g]
+            grouped = work.tile([P, 4 * 4 * P], BF16, align_bytes=64, name="x_grouped", tag="xg")
+            for s in range(0, n1 - n0, 2):
+                turn_pair(x_raw[g], list(range(s, min(s + 2, n1 - n0))), grouped, s * P)
+            cols = slice(n0 * P, n1 * P)
+            nc.vector.quantize_mx(
+                out=x_codes[:, cols].bitcast(FP8X4), scales=x_scales[:, cols], in_=grouped[:, 0 : (n1 - n0) * P * 4]
+            )
+
+        def prepare_q():
+            grouped = work.tile([P, 4 * Q], BF16, align_bytes=64, name="q_grouped", tag="xg")
+            signed = work.tile([P, 4 * Q], BF16, align_bytes=64, name="q_signed", tag="wg")
+            for s in range(0, T, 2):
+                turn_pair(q_raw, [s, s + 1], grouped, s * P)
+            nc.vector.tensor_tensor(
+                out=signed[:].rearrange("p (c j) -> p c j", j=4),
+                in0=grouped[:].rearrange("p (c j) -> p c j", j=4),
+                in1=sign[:].unsqueeze(1).to_broadcast([P, Q, 4]),
+                op=ALU.mult,
+            )
+            nc.vector.quantize_mx(out=q_codes[:].bitcast(FP8X4), scales=q_scales[:], in_=signed[:])
+
+        def convolve(j):
+            d_sep = work.tile([P, T, BLK], BF16, name="d_sep", tag="ds")
+            for t in range(T):
+                bank = spsum.tile([P, BLK], F32, name="h_bank", tag="s")
+                for s in range(2):
+                    cols = slice(j * BLK + s * P, j * BLK + s * P + BLK)
+                    nc.tensor.matmul_mx(
+                        out=bank[:],
+                        lhsT=w_codes[s][:, t * P : (t + 1) * P].bitcast(FP8X4),
+                        lhsT_scale=w_scales[s][:, t * P : (t + 1) * P],
+                        rhs=x_codes[:, cols].bitcast(FP8X4),
+                        rhs_scale=x_scales[:, cols],
+                        start=(s == 0),
+                        stop=(s == 1),
+                    )
+                nc.scalar.activation(
+                    out=d_sep[:, t, :], in_=bank[:], func=ACT.Relu, bias=gain_bias[:, t : t + 1], scale=gain_abs[:, t : t + 1]
+                )
+            grouped = work.tile([P, 4 * BLK], BF16, align_bytes=64, name="d_grouped", tag="dg")
+            nc.vector.tensor_copy(
+                out=grouped[:].rearrange("p (c t) -> p c t", t=T), in_=d_sep[:].rearrange("p t c -> p c t")
+            )
+            cols = slice(j * BLK, (j + 1) * BLK)
+            nc.vector.quantize_mx(out=d_codes[:, cols].bitcast(FP8X4), scales=d_scales[:, cols], in_=grouped[:])
+
+        s_banks = {}
+
+        def score(t, j):
+            bank = spsum.tile([P, BLK], F32, name="s_bank", tag="s")
+            cols = slice(j * BLK, (j + 1) * BLK)
+            nc.tensor.matmul_mx(
+                out=bank[:],
+                lhsT=q_codes[:, t * P : (t + 1) * P].bitcast(FP8X4),
+                lhsT_scale=q_scales[:, t * P : (t + 1) * P],
+                rhs=d_codes[:, cols].bitcast(FP8X4),
+                rhs_scale=d_scales[:, cols],
+                start=True,
+                stop=True,
+            )
+            s_banks[t, j] = bank
+
+        y_tiles = {}
+        negr = keep.tile([P, T, K, B], F32, name="negr")
+        sums = keep.tile([P, T, K, B], F32, name="sums")
+
+        def square(u, j):
+            t, k = divmod(u, K)
+            if j == 0:
+                y_tiles[u] = ypool.tile([P, N * B], F32, name="y", tag="y")
+            nc.scalar.activation(
+                out=y_tiles[u][:, j * BLK : (j + 1) * BLK],
+                in_=s_banks[t, j][:],
+                func=ACT.Square,
+                bias=z_bias[:, k : k + 1],
+                scale=z_scale[:, k : k + 1],
+            )
+
+        def nearest(u):
+            t, k = divmod(u, K)
+            y = y_tiles[u]
+            m1 = work.tile([P, 1024], F32, name="m1", tag="m1")
+            m2 = work.tile([P, 512], F32, name="m2", tag="m2")
+            nc.vector.tensor_tensor(out=m1[:], in0=y[:, 0:1024], in1=y[:, 1024:2048], op=ALU.min)
+            nc.vector.tensor_tensor(out=m2[:], in0=m1[:, 0:512], in1=m1[:, 512:1024], op=ALU.min)
+            nc.vector.tensor_reduce(
+                out=negr[:, t, k, :], in_=m2[:].rearrange("p (n b) -> p b n", n=4), axis=AX.X, op=ALU.min, negate=True
+            )
+
+        e_tiles = {}
+
+        def exponent(u, j):
+            t, k = divmod(u, K)
+            bank = xpsum.tile([P, NB, P], F32, name="a_bank", tag="xb")
+            for i in range(NB):
+                n = j * NB + i
+                nc.tensor.matmul(bank[:, i, :], lhsT=y_tiles[u][:, n * B : (n + 1) * B], rhs=ident[:], is_transpose=True, start=True, stop=False)
+                nc.tensor.matmul(bank[:, i, :], lhsT=negr[:, t, k, :], rhs=ident[:], is_transpose=True, start=False, stop=True)
+            e = epool.tile([P, NB, P], F32, name="e", tag="e")
+            nc.scalar.activation(out=e[:], in_=bank[:], func=ACT.Exp, scale=-1.0)
+            e_tiles[u, j] = e
+
+        sum_banks = {}
+
+        def add_up(u, j):
+            t, k = divmod(u, K)
+            if j == 0:
+                sum_banks[u] = upsum.tile([P, P], F32, name="sum_bank", tag="u")
+            for i in range(NB):
+                n = j * NB + i
+                nc.tensor.matmul(sum_banks[u][:], lhsT=e_tiles[u, j][:, i, :], rhs=ident[:], is_transpose=True, start=(n == 0), stop=(n == N - 1))
+            if j == NB - 1:
+                nc.vector.tensor_copy(out=sums[:, t, k, :], in_=sum_banks[u][:])
+
+        prepare_x(0)
+        prepare_x(1)
+        prepare_w(0)
+        prepare_w(1)
+        convolve(0)
+        prepare_q()
+        prepare_x(2)
+        score(0, 0)
+        square(0, 0)
+        square(1, 0)
+        for j in range(1, 4):
+            convolve(j)
+            if j < 3:
+                prepare_x(j + 2)
+            score(0, j)
+            square(0, j)
+            square(1, j)
+
+        units = T * K
+        nearest(0)
+        for u in range(units + 1):
+            if u + 1 < units:
+                nearest(u + 1)
+            for j in range(4):
+                if u < units:
+                    exponent(u, j)
+                if u + 2 < units:
+                    t2, k2 = divmod(u + 2, K)
+                    if k2 == 0:
+                        score(t2, j)
+                    square(u + 2, j)
+                if u >= 1:
+                    add_up(u - 1, j)
+
+        logs = keep.tile([P, T, K, B], F32, name="logs")
+        res = keep.tile([P, T, B * K], F32, name="res")
+        for t in range(T):
+            nc.scalar.activation(out=logs[:, t], in_=sums[:, t], func=ACT.Ln, scale=1.0 / N)
+            nc.vector.tensor_tensor(
+                out=res[:, t, :].rearrange("p (b k) -> p b k", k=K),
+                in0=logs[:, t].rearrange("p k b -> p b k"),
+                in1=negr[:, t].rearrange("p k b -> p b k"),
+                op=ALU.add,
+            )
+        nc.sync.dma_start(out=out_0.rearrange("(p t) b k -> p t (b k)", t=T), in_=res[:])
+        o_codes = keep.tile([P, B * K], U32, align_bytes=64, name="o_codes")
+        o_scales = keep.tile([P, B * K], U8, align_bytes=64, name="o_scales")
+        o_grouped = keep.tile([P, B * K * T], BF16, align_bytes=64, name="o_grouped")
+        for c0, c1 in ((0, 512), (512, 768)):
+            src = res[:, :, c0:c1].rearrange("p t c -> p c t")
+            dst = o_grouped[:, c0 * T : c1 * T].rearrange("p (c t) -> p c t", t=T)
+            if c0 == 0:
+                nc.vector.tensor_copy(out=dst, in_=src)
+            else:
+                nc.scalar.copy(out=dst, in_=src)
+            nc.vector.quantize_mx(out=o_codes[:, c0:c1].bitcast(FP8X4), scales=o_scales[:, c0:c1], in_=o_grouped[:, c0 * T : c1 * T])
+        nc.sync.dma_start(out=out_1[0].rearrange("p m t -> p (m t)").bitcast(I32), in_=o_codes[:].bitcast(I32))
+        for g in range(4):
+            nc.sync.dma_start(out=out_2[0, 4 * g : 4 * g + 4, :].bitcast(I32), in_=o_scales[32 * g : 32 * g + 4, :].bitcast(I32))

@@ -21,67 +21,60 @@ P = 128
 T = 4
 BLK = 512
 NB = 4
+ON_SCALAR = [[1,0,1,1],[1,0,1,1],[1,0,1,1],[1,0,1,1]]
+UNITS = T * K
+AHEAD = 5
 
 
 def tile_bigramconvkernelpoolingmatch_x1_kernel(tc, q, x, w, bias, gain, mu, sigma, out_0, out_1, out_2):
     nc = tc.nc
     with ExitStack() as ctx:
+        ctx.enter_context(tc.manual_schedule())
         keep = ctx.enter_context(tc.tile_pool(name="keep", bufs=1))
         work = ctx.enter_context(tc.tile_pool(name="work", bufs=2))
-        ypool = ctx.enter_context(tc.tile_pool(name="ypool", bufs=5))
-        epool = ctx.enter_context(tc.tile_pool(name="epool", bufs=8))
+        ypool = ctx.enter_context(tc.tile_pool(name="ypool", bufs=9))
         spsum = ctx.enter_context(tc.psum_pool(name="spsum", bufs=4))
-        xpsum = ctx.enter_context(tc.psum_pool(name="xpsum", bufs=3))
-        upsum = ctx.enter_context(tc.psum_pool(name="upsum", bufs=1))
-
-        x_groups = [(0, 1), (1, 5), (5, 9), (9, 13), (13, 17)]
-        x_raw = []
-        for g, (n0, n1) in enumerate(x_groups):
-            x_raw.append(keep.tile([P, (n1 - n0) * D], BF16, name="x_raw%d" % g))
-        w_raw = []
-        for s in range(2):
-            w_raw.append(keep.tile([P, 4, E], BF16, name="w_raw%d" % s))
-        q_raw = keep.tile([P, T * E], BF16, name="q_raw")
-
-        def load_x(g):
-            n0, n1 = x_groups[g]
-            nc.sync.dma_start(out=x_raw[g][:], in_=x[:, n0:n1, :].rearrange("b n d -> b (n d)"))
+        xpsum = ctx.enter_context(tc.psum_pool(name="xpsum", bufs=2))
+        upsum = ctx.enter_context(tc.psum_pool(name="upsum", bufs=2))
 
         gain_sb = keep.tile([P, 4], BF16, name="gain_sb")
         bias_sb = keep.tile([P, 4], BF16, name="bias_sb")
         mu_sb = keep.tile([P, K], BF16, name="mu_sb")
         sigma_sb = keep.tile([P, K], BF16, name="sigma_sb")
-
-        load_x(0)
-        load_x(1)
-        nc.sync.dma_start(out=w_raw[0][:], in_=w[0].rearrange("(p j) c -> p j c", j=4))
-        nc.sync.dma_start(out=w_raw[1][:], in_=w[1].rearrange("(p j) c -> p j c", j=4))
         nc.scalar.dma_start(out=gain_sb[:], in_=gain.rearrange("(p t) -> p t", t=4))
         nc.scalar.dma_start(out=bias_sb[:], in_=bias.rearrange("(p t) -> p t", t=4))
         nc.scalar.dma_start(out=mu_sb[:], in_=mu.partition_broadcast(P))
         nc.scalar.dma_start(out=sigma_sb[:], in_=sigma.partition_broadcast(P))
+
+        x_groups = [(0, 1), (1, 5), (5, 9), (9, 13), (13, 17)]
+        x_raw = {}
+
+        def load_x(g):
+            n0, n1 = x_groups[g]
+            x_raw[g] = work.tile([P, (n1 - n0) * D], BF16, name="x_raw", tag="x0" if g == 0 else "xr", bufs=1 if g == 0 else 3)
+            nc.sync.dma_start(out=x_raw[g][:], in_=x[:, n0:n1, :].rearrange("b n d -> b (n d)"))
+
+        w_raw = []
+        for s in range(2):
+            w_raw.append(keep.tile([P, 4, E], BF16, name="w_raw%d" % s))
+        q_raw = keep.tile([P, T * E], BF16, name="q_raw")
+
+        def load_w(s):
+            nc.sync.dma_start(out=w_raw[s][:], in_=w[s].rearrange("(p j) c -> p j c", j=4))
+
+        def load_q():
+            nc.sync.dma_start(out=q_raw[:], in_=q.rearrange("(m t) k -> m (t k)", t=T))
+
+        load_x(0)
+        load_x(1)
+        load_w(0)
         load_x(2)
-        nc.sync.dma_start(out=q_raw[:], in_=q.rearrange("(m t) k -> m (t k)", t=T))
+        load_w(1)
         load_x(3)
-        load_x(4)
+        load_q()
 
         ident = keep.tile([P, P], F32, name="ident")
         make_identity(nc, ident[:])
-
-        gain_abs = keep.tile([P, 4], F32, name="gain_abs")
-        gain_bias = keep.tile([P, 4], F32, name="gain_bias")
-        sign01 = keep.tile([P, 4], F32, name="sign01")
-        sign = keep.tile([P, 4], BF16, name="sign")
-        nc.scalar.activation(out=gain_abs[:], in_=gain_sb[:], func=ACT.Abs)
-        nc.vector.tensor_tensor(out=gain_bias[:], in0=gain_abs[:], in1=bias_sb[:], op=ALU.mult)
-        nc.vector.tensor_scalar(out=sign01[:], in0=gain_sb[:], scalar1=0.0, scalar2=2.0, op0=ALU.is_ge, op1=ALU.mult)
-        nc.vector.tensor_scalar(out=sign[:], in0=sign01[:], scalar1=1.0, scalar2=None, op0=ALU.subtract)
-        z_scale = keep.tile([P, K], F32, name="z_scale")
-        z_bias = keep.tile([P, K], F32, name="z_bias")
-        rsig = keep.tile([P, K], F32, name="rsig")
-        nc.vector.reciprocal(out=rsig[:], in_=sigma_sb[:])
-        nc.vector.tensor_scalar(out=z_scale[:], in0=rsig[:], scalar1=0.7071067811865476, scalar2=None, op0=ALU.mult)
-        nc.vector.scalar_tensor_tensor(out=z_bias[:], in0=mu_sb[:], scalar=-1.0, in1=z_scale[:], op0=ALU.mult, op1=ALU.mult)
 
         w_codes = []
         w_scales = []
@@ -100,56 +93,90 @@ def tile_bigramconvkernelpoolingmatch_x1_kernel(tc, q, x, w, bias, gain, mu, sig
             for u in range(2):
                 nc.tensor.transpose(bank[:, place, u, :], words[:, u : D // 2 : 2], ident[:])
 
-        def turn_pair(raw, slots, grouped, first_col):
-            bank = xpsum.tile([P, 2, 2, P], F32, name="x_bank", tag="xb")
-            for place, slot in enumerate(slots):
-                transpose_words(raw, slot, bank, place)
-            n = len(slots)
-            cols = slice(first_col * 4, (first_col + n * P) * 4)
+        turn_banks = {}
+
+        def turn_pair(raw, first, n, key):
+            bank = spsum.tile([P, 2, 2, P], F32, name="x_bank", tag="s")
+            for place in range(n):
+                transpose_words(raw, first + place, bank, place)
+            turn_banks[key] = bank
+
+        def copy_pair(grouped, first, n, key):
+            cols = slice(first * P * 4, (first + n) * P * 4)
             nc.scalar.copy(
                 out=grouped[:, cols].bitcast(F32).rearrange("p (n r u) -> p n r u", n=n, u=2),
-                in_=bank[:, 0:n].rearrange("p n u r -> p n r u"),
+                in_=turn_banks[key][:, 0:n].rearrange("p n u r -> p n r u"),
             )
 
-        def prepare_w(s):
-            grouped = work.tile([P, 4 * E], BF16, align_bytes=64, name="w_grouped", tag="wg")
+        w_grouped = {}
+
+        def interleave_w(s):
+            w_grouped[s] = work.tile([P, 4 * E], BF16, align_bytes=64, name="w_grouped", tag="wg")
             nc.vector.tensor_copy(
-                out=grouped[:].rearrange("p (t m j) -> p t m j", t=4, j=4),
+                out=w_grouped[s][:].rearrange("p (t m j) -> p t m j", t=4, j=4),
                 in_=w_raw[s][:].rearrange("p j (m t) -> p t m j", t=4),
             )
-            nc.vector.quantize_mx(out=w_codes[s][:].bitcast(FP8X4), scales=w_scales[s][:], in_=grouped[:])
 
-        def prepare_x(g):
+        def quantise_w(s):
+            nc.vector.quantize_mx(out=w_codes[s][:].bitcast(FP8X4), scales=w_scales[s][:], in_=w_grouped[s][:])
+
+        x_grouped = {}
+
+        def turn_x(g, s):
             n0, n1 = x_groups[g]
-            grouped = work.tile([P, 4 * 4 * P], BF16, align_bytes=64, name="x_grouped", tag="xg")
-            for s in range(0, n1 - n0, 2):
-                turn_pair(x_raw[g], list(range(s, min(s + 2, n1 - n0))), grouped, s * P)
+            turn_pair(x_raw[g], s, min(2, n1 - n0 - s), ("x", g, s))
+
+        def copy_x(g, s):
+            n0, n1 = x_groups[g]
+            if s == 0:
+                x_grouped[g] = work.tile([P, 4 * 4 * P], BF16, align_bytes=64, name="x_grouped", tag="xg")
+            copy_pair(x_grouped[g], s, min(2, n1 - n0 - s), ("x", g, s))
+
+        def quantise_x(g):
+            n0, n1 = x_groups[g]
             cols = slice(n0 * P, n1 * P)
             nc.vector.quantize_mx(
-                out=x_codes[:, cols].bitcast(FP8X4), scales=x_scales[:, cols], in_=grouped[:, 0 : (n1 - n0) * P * 4]
+                out=x_codes[:, cols].bitcast(FP8X4), scales=x_scales[:, cols], in_=x_grouped[g][:, 0 : (n1 - n0) * P * 4]
             )
 
-        def prepare_q():
-            grouped = work.tile([P, 4 * Q], BF16, align_bytes=64, name="q_grouped", tag="xg")
-            signed = work.tile([P, 4 * Q], BF16, align_bytes=64, name="q_signed", tag="wg")
-            for s in range(0, T, 2):
-                turn_pair(q_raw, [s, s + 1], grouped, s * P)
+        q_tiles = {}
+
+        def turn_q(s):
+            turn_pair(q_raw, s, 2, ("q", s))
+
+        def copy_q(s):
+            if s == 0:
+                q_tiles["grouped"] = work.tile([P, 4 * Q], BF16, align_bytes=64, name="q_grouped", tag="qg", bufs=1)
+            copy_pair(q_tiles["grouped"], s, 2, ("q", s))
+
+        def sign_q():
+            q_tiles["signed"] = work.tile([P, 4 * Q], BF16, align_bytes=64, name="q_signed", tag="wg")
             nc.vector.tensor_tensor(
-                out=signed[:].rearrange("p (c j) -> p c j", j=4),
-                in0=grouped[:].rearrange("p (c j) -> p c j", j=4),
+                out=q_tiles["signed"][:].rearrange("p (c j) -> p c j", j=4),
+                in0=q_tiles["grouped"][:].rearrange("p (c j) -> p c j", j=4),
                 in1=sign[:].unsqueeze(1).to_broadcast([P, Q, 4]),
                 op=ALU.mult,
             )
-            nc.vector.quantize_mx(out=q_codes[:].bitcast(FP8X4), scales=q_scales[:], in_=signed[:])
+
+        def quantise_q():
+            nc.vector.quantize_mx(out=q_codes[:].bitcast(FP8X4), scales=q_scales[:], in_=q_tiles["signed"][:])
+
+        d_sep = {}
+
+        h_banks = {}
 
         def convolve(j):
-            d_sep = work.tile([P, T, BLK], BF16, name="d_sep", tag="ds")
             for t in range(T):
-                bank = spsum.tile([P, BLK], F32, name="h_bank", tag="s")
-                for s in range(2):
-                    cols = slice(j * BLK + s * P, j * BLK + s * P + BLK)
+                if t < 2:
+                    h_bank = xpsum.tile([P, BLK], F32, name="h_bank", tag="xb")
+                else:
+                    h_bank = upsum.tile([P, BLK], F32, name="h_bank", tag="u")
+                h_banks[j, t] = h_bank
+            for s in range(2):
+                cols = slice(j * BLK + s * P, j * BLK + s * P + BLK)
+                for t in range(T):
                     nc.tensor.matmul_mx(
-                        out=bank[:],
+                        out=h_banks[j, t][:],
                         lhsT=w_codes[s][:, t * P : (t + 1) * P].bitcast(FP8X4),
                         lhsT_scale=w_scales[s][:, t * P : (t + 1) * P],
                         rhs=x_codes[:, cols].bitcast(FP8X4),
@@ -157,140 +184,302 @@ def tile_bigramconvkernelpoolingmatch_x1_kernel(tc, q, x, w, bias, gain, mu, sig
                         start=(s == 0),
                         stop=(s == 1),
                     )
-                nc.scalar.activation(
-                    out=d_sep[:, t, :], in_=bank[:], func=ACT.Relu, bias=gain_bias[:, t : t + 1], scale=gain_abs[:, t : t + 1]
-                )
-            grouped = work.tile([P, 4 * BLK], BF16, align_bytes=64, name="d_grouped", tag="dg")
-            nc.vector.tensor_copy(
-                out=grouped[:].rearrange("p (c t) -> p c t", t=T), in_=d_sep[:].rearrange("p t c -> p c t")
-            )
-            cols = slice(j * BLK, (j + 1) * BLK)
-            nc.vector.quantize_mx(out=d_codes[:, cols].bitcast(FP8X4), scales=d_scales[:, cols], in_=grouped[:])
 
-        s_banks = {}
+        def rectify(j, t):
+            if t == 0:
+                d_sep[j] = work.tile([P, T, BLK], BF16, name="d_sep", tag="ds")
+            if ON_SCALAR[j][t]:
+                nc.scalar.activation(
+                    out=d_sep[j][:, t, :], in_=h_banks[j, t][:], func=ACT.Identity, bias=gain_bias[:, t : t + 1], scale=gain_abs[:, t : t + 1]
+                )
+            else:
+                nc.vector.tensor_scalar(
+                    out=d_sep[j][:, t, :], in0=h_banks[j, t][:], scalar1=gain_abs[:, t : t + 1], scalar2=gain_bias[:, t : t + 1], op0=ALU.mult, op1=ALU.add
+                )
+
+        d_grouped = {}
+
+        def interleave_d(j):
+            d_grouped[j] = work.tile([P, 4 * BLK], BF16, align_bytes=64, name="d_grouped", tag="dg")
+            nc.vector.tensor_scalar(
+                out=d_grouped[j][:].rearrange("p (c t) -> p c t", t=T),
+                in0=d_sep[j][:].rearrange("p t c -> p c t"),
+                scalar1=0.0,
+                scalar2=None,
+                op0=ALU.max,
+            )
+
+        def quantise_d(j):
+            cols = slice(j * BLK, (j + 1) * BLK)
+            nc.vector.quantize_mx(out=d_codes[:, cols].bitcast(FP8X4), scales=d_scales[:, cols], in_=d_grouped[j][:])
+
+        score_banks = {}
 
         def score(t, j):
             bank = spsum.tile([P, BLK], F32, name="s_bank", tag="s")
-            cols = slice(j * BLK, (j + 1) * BLK)
-            nc.tensor.matmul_mx(
-                out=bank[:],
-                lhsT=q_codes[:, t * P : (t + 1) * P].bitcast(FP8X4),
-                lhsT_scale=q_scales[:, t * P : (t + 1) * P],
-                rhs=d_codes[:, cols].bitcast(FP8X4),
-                rhs_scale=d_scales[:, cols],
-                start=True,
-                stop=True,
-            )
-            s_banks[t, j] = bank
+            for i in range(NB):
+                cols = slice((j * NB + i) * B, (j * NB + i + 1) * B)
+                nc.tensor.matmul_mx(
+                    out=bank[:, i * P : (i + 1) * P],
+                    lhsT=d_codes[:, cols].bitcast(FP8X4),
+                    lhsT_scale=d_scales[:, cols],
+                    rhs=q_codes[:, t * P : (t + 1) * P].bitcast(FP8X4),
+                    rhs_scale=q_scales[:, t * P : (t + 1) * P],
+                    start=True,
+                    stop=True,
+                )
+            score_banks[j] = bank
 
         y_tiles = {}
-        negr = keep.tile([P, T, K, B], F32, name="negr")
-        sums = keep.tile([P, T, K, B], F32, name="sums")
 
         def square(u, j):
-            t, k = divmod(u, K)
+            k = u % K
             if j == 0:
-                y_tiles[u] = ypool.tile([P, N * B], F32, name="y", tag="y")
+                y_tiles[u] = ypool.tile([P, N * P], F32, name="y", tag="y")
             nc.scalar.activation(
                 out=y_tiles[u][:, j * BLK : (j + 1) * BLK],
-                in_=s_banks[t, j][:],
+                in_=score_banks[j][:],
                 func=ACT.Square,
                 bias=z_bias[:, k : k + 1],
                 scale=z_scale[:, k : k + 1],
             )
 
-        def nearest(u):
-            t, k = divmod(u, K)
-            y = y_tiles[u]
-            m1 = work.tile([P, 1024], F32, name="m1", tag="m1")
-            m2 = work.tile([P, 512], F32, name="m2", tag="m2")
-            nc.vector.tensor_tensor(out=m1[:], in0=y[:, 0:1024], in1=y[:, 1024:2048], op=ALU.min)
-            nc.vector.tensor_tensor(out=m2[:], in0=m1[:, 0:512], in1=m1[:, 512:1024], op=ALU.min)
-            nc.vector.tensor_reduce(
-                out=negr[:, t, k, :], in_=m2[:].rearrange("p (n b) -> p b n", n=4), axis=AX.X, op=ALU.min, negate=True
-            )
+        r_tiles = {}
+        part = {}
 
-        e_tiles = {}
+        def nearest(u, step):
+            width = 1024 >> step
+            source = y_tiles[u][:] if step == 0 else part[u]
+            if step < 3:
+                m = work.tile([P, width], F32, name="m%d" % step, tag="m%d" % step)
+            else:
+                m = work.tile([P, width], F32, name="r", tag="r", bufs=4)
+                r_tiles[u] = m
+            nc.vector.tensor_tensor(out=m[:], in0=source[:, 0:width], in1=source[:, width : 2 * width], op=ALU.min)
+            part[u] = m[:]
 
-        def exponent(u, j):
-            t, k = divmod(u, K)
-            bank = xpsum.tile([P, NB, P], F32, name="a_bank", tag="xb")
-            for i in range(NB):
-                n = j * NB + i
-                nc.tensor.matmul(bank[:, i, :], lhsT=y_tiles[u][:, n * B : (n + 1) * B], rhs=ident[:], is_transpose=True, start=True, stop=False)
-                nc.tensor.matmul(bank[:, i, :], lhsT=negr[:, t, k, :], rhs=ident[:], is_transpose=True, start=False, stop=True)
-            e = epool.tile([P, NB, P], F32, name="e", tag="e")
-            nc.scalar.activation(out=e[:], in_=bank[:], func=ACT.Exp, scale=-1.0)
-            e_tiles[u, j] = e
+        def subtract(u, h):
+            y = y_tiles[u][:, h * 1024 : (h + 1) * 1024].rearrange("p (n i) -> p n i", n=8)
+            nc.vector.tensor_tensor(out=y, in0=y, in1=r_tiles[u][:].unsqueeze(1).to_broadcast([P, 8, P]), op=ALU.subtract)
+
+        def exponent(u, first, last):
+            y = y_tiles[u][:, first * BLK : last * BLK]
+            nc.scalar.activation(out=y, in_=y, func=ACT.Exp, scale=-1.0)
 
         sum_banks = {}
 
         def add_up(u, j):
-            t, k = divmod(u, K)
             if j == 0:
-                sum_banks[u] = upsum.tile([P, P], F32, name="sum_bank", tag="u")
-            for i in range(NB):
-                n = j * NB + i
-                nc.tensor.matmul(sum_banks[u][:], lhsT=e_tiles[u, j][:, i, :], rhs=ident[:], is_transpose=True, start=(n == 0), stop=(n == N - 1))
-            if j == NB - 1:
-                nc.vector.tensor_copy(out=sums[:, t, k, :], in_=sum_banks[u][:])
+                sum_banks[u] = upsum.tile([P, 2, P], F32, name="sum_bank", tag="u")
+                nc.tensor.transpose(sum_banks[u][:, 1, :], r_tiles[u][:], ident[:])
+            for n in range(j * NB, (j + 1) * NB):
+                nc.tensor.matmul(
+                    sum_banks[u][:, 0, :],
+                    lhsT=y_tiles[u][:, n * P : (n + 1) * P],
+                    rhs=ident[:],
+                    is_transpose=True,
+                    start=(n == 0),
+                    stop=(n == N - 1),
+                )
 
-        prepare_x(0)
-        prepare_x(1)
-        prepare_w(0)
-        prepare_w(1)
+        stats = {}
+
+        reordered = keep.tile([P, T - 1, 2, B * K], F32, name="reordered")
+
+        def take_sum(u):
+            t, k = divmod(u, K)
+            if k == 0:
+                stats[t] = work.tile([P, 2, K, B], F32, name="stats", tag="st")
+            if u % 2 == 1 and u < UNITS - 2:
+                nc.scalar.copy(out=stats[t][:, :, k, :], in_=sum_banks[u][:])
+            else:
+                nc.vector.tensor_copy(out=stats[t][:, :, k, :], in_=sum_banks[u][:])
+            if k == K - 1 and t < T - 1:
+                nc.gpsimd.tensor_scalar(
+                    out=reordered[:, t].rearrange("p s (b k) -> p s b k", k=K),
+                    in0=stats[t][:].rearrange("p s k b -> p s b k"),
+                    scalar1=1.0,
+                    scalar2=0.0,
+                    op0=ALU.mult,
+                    op1=ALU.add,
+                )
+
+        gain_neg = keep.tile([P, 4], F32, name="gain_neg")
+        gain_abs = keep.tile([P, 4], F32, name="gain_abs")
+        gain_bias = keep.tile([P, 4], F32, name="gain_bias")
+        sign01 = keep.tile([P, 4], F32, name="sign01")
+        sign = keep.tile([P, 4], BF16, name="sign")
+        z_scale = keep.tile([P, K], F32, name="z_scale")
+        z_bias = keep.tile([P, K], F32, name="z_bias")
+        rsig = keep.tile([P, K], F32, name="rsig")
+        nc.vector.tensor_scalar(out=gain_neg[:], in0=gain_sb[:], scalar1=-1.0, scalar2=None, op0=ALU.mult)
+        nc.vector.reciprocal(out=rsig[:], in_=sigma_sb[:])
+        nc.vector.tensor_tensor(out=gain_abs[:], in0=gain_sb[:], in1=gain_neg[:], op=ALU.max)
+        nc.vector.tensor_scalar(out=z_scale[:], in0=rsig[:], scalar1=0.7071067811865476, scalar2=None, op0=ALU.mult)
+        nc.vector.tensor_tensor(out=gain_bias[:], in0=gain_abs[:], in1=bias_sb[:], op=ALU.mult)
+        nc.vector.scalar_tensor_tensor(out=z_bias[:], in0=mu_sb[:], scalar=-1.0, in1=z_scale[:], op0=ALU.mult, op1=ALU.mult)
+        nc.vector.tensor_scalar(out=sign01[:], in0=gain_sb[:], scalar1=0.0, scalar2=2.0, op0=ALU.is_ge, op1=ALU.mult)
+        nc.vector.tensor_scalar(out=sign[:], in0=sign01[:], scalar1=1.0, scalar2=None, op0=ALU.subtract)
+
+        turn_x(0, 0)
+        copy_x(0, 0)
+        turn_x(1, 0)
+        turn_x(1, 2)
+        copy_x(1, 0)
+        copy_x(1, 2)
+        interleave_w(0)
+        quantise_x(0)
+        quantise_x(1)
+        quantise_w(0)
+        turn_x(2, 0)
+        turn_x(2, 2)
+        copy_x(2, 0)
+        copy_x(2, 2)
+        interleave_w(1)
+        quantise_w(1)
+        quantise_x(2)
+        load_x(4)
+        turn_x(3, 0)
+        turn_x(3, 2)
+        copy_x(3, 0)
+        copy_x(3, 2)
         convolve(0)
-        prepare_q()
-        prepare_x(2)
+        rectify(0, 0)
+        rectify(0, 1)
+        rectify(0, 2)
+        rectify(0, 3)
+        turn_q(0)
+        turn_q(2)
+        copy_q(0)
+        copy_q(2)
+        interleave_d(0)
+        quantise_x(3)
+        quantise_d(0)
+        convolve(1)
+        rectify(1, 0)
+        rectify(1, 1)
+        rectify(1, 2)
+        rectify(1, 3)
+        turn_x(4, 0)
+        turn_x(4, 2)
+        copy_x(4, 0)
+        copy_x(4, 2)
+        sign_q()
+        interleave_d(1)
+        quantise_x(4)
+        quantise_d(1)
+        convolve(2)
+        rectify(2, 0)
+        rectify(2, 1)
+        rectify(2, 2)
+        rectify(2, 3)
+        quantise_q()
         score(0, 0)
         square(0, 0)
         square(1, 0)
-        for j in range(1, 4):
-            convolve(j)
-            if j < 3:
-                prepare_x(j + 2)
-            score(0, j)
-            square(0, j)
-            square(1, j)
+        interleave_d(2)
+        quantise_d(2)
+        convolve(3)
+        score(0, 1)
+        rectify(3, 0)
+        rectify(3, 1)
+        rectify(3, 2)
+        rectify(3, 3)
+        square(0, 1)
+        square(1, 1)
+        score(0, 2)
+        square(0, 2)
+        interleave_d(3)
+        quantise_d(3)
+        score(0, 3)
+        square(1, 2)
+        square(0, 3)
+        square(1, 3)
+        square(2, 0)
+        square(2, 1)
+        square(2, 2)
+        square(2, 3)
+        square(3, 0)
+        square(3, 1)
+        square(3, 2)
+        square(3, 3)
+        square(4, 0)
+        square(4, 1)
+        square(4, 2)
+        square(4, 3)
 
-        units = T * K
-        nearest(0)
-        for u in range(units + 1):
-            if u + 1 < units:
-                nearest(u + 1)
-            for j in range(4):
-                if u < units:
-                    exponent(u, j)
-                if u + 2 < units:
-                    t2, k2 = divmod(u + 2, K)
-                    if k2 == 0:
-                        score(t2, j)
-                    square(u + 2, j)
-                if u >= 1:
+        squares = [(u, j) for u in range(AHEAD, UNITS) for j in range(4)]
+
+        def next_square():
+            if squares:
+                u, j = squares.pop(0)
+                if u % K == 0:
+                    score(u // K, j)
+                square(u, j)
+
+        for step in range(4):
+            nearest(0, step)
+            nearest(1, step)
+        subtract(0, 0)
+        subtract(0, 1)
+        for u in range(UNITS):
+            if u + 2 < UNITS:
+                nearest(u + 2, 0)
+            if u + 1 < UNITS:
+                subtract(u + 1, 0)
+            if u + 2 < UNITS:
+                nearest(u + 2, 1)
+            if u + 1 < UNITS:
+                subtract(u + 1, 1)
+            if u + 2 < UNITS:
+                nearest(u + 2, 2)
+            if u >= 2:
+                take_sum(u - 2)
+            if u + 2 < UNITS:
+                nearest(u + 2, 3)
+            if 1 <= u < UNITS - 1:
+                for j in range(4):
                     add_up(u - 1, j)
+            if u < UNITS - 2:
+                exponent(u, 0, 4)
+            else:
+                for j in range(4):
+                    exponent(u, j, j + 1)
+                    add_up(u, j)
+            for i in range(4):
+                next_square()
+        take_sum(UNITS - 2)
+        take_sum(UNITS - 1)
 
-        logs = keep.tile([P, T, K, B], F32, name="logs")
         res = keep.tile([P, T, B * K], F32, name="res")
+        last = stats[T - 1]
+        for t in range(T - 1):
+            nc.scalar.activation(out=reordered[:, t, 0, :], in_=reordered[:, t, 0, :], func=ACT.Ln, scale=1.0 / N)
+        nc.scalar.activation(out=last[:, 0, 0 : K - 1], in_=last[:, 0, 0 : K - 1], func=ACT.Ln, scale=1.0 / N)
+        nc.scalar.activation(out=last[:, 0, K - 1], in_=last[:, 0, K - 1], func=ACT.Ln, scale=1.0 / N)
         for t in range(T):
-            nc.scalar.activation(out=logs[:, t], in_=sums[:, t], func=ACT.Ln, scale=1.0 / N)
-            nc.vector.tensor_tensor(
-                out=res[:, t, :].rearrange("p (b k) -> p b k", k=K),
-                in0=logs[:, t].rearrange("p k b -> p b k"),
-                in1=negr[:, t].rearrange("p k b -> p b k"),
-                op=ALU.add,
-            )
-        nc.sync.dma_start(out=out_0.rearrange("(p t) b k -> p t (b k)", t=T), in_=res[:])
+            if t < T - 1:
+                nc.vector.tensor_tensor(out=res[:, t, :], in0=reordered[:, t, 0], in1=reordered[:, t, 1], op=ALU.subtract)
+            else:
+                nc.vector.tensor_tensor(
+                    out=res[:, t, :].rearrange("p (b k) -> p b k", k=K),
+                    in0=last[:, 0].rearrange("p k b -> p b k"),
+                    in1=last[:, 1].rearrange("p k b -> p b k"),
+                    op=ALU.subtract,
+                )
+            nc.sync.dma_start(out=out_0.rearrange("(p t) b k -> p t (b k)", t=T)[:, t, :], in_=res[:, t, :])
         o_codes = keep.tile([P, B * K], U32, align_bytes=64, name="o_codes")
         o_scales = keep.tile([P, B * K], U8, align_bytes=64, name="o_scales")
-        o_grouped = keep.tile([P, B * K * T], BF16, align_bytes=64, name="o_grouped")
         for c0, c1 in ((0, 512), (512, 768)):
+            o_grouped = work.tile([P, 4 * BLK], BF16, align_bytes=64, name="o_grouped", tag="dg")
             src = res[:, :, c0:c1].rearrange("p t c -> p c t")
-            dst = o_grouped[:, c0 * T : c1 * T].rearrange("p (c t) -> p c t", t=T)
+            dst = o_grouped[:, 0 : (c1 - c0) * T].rearrange("p (c t) -> p c t", t=T)
             if c0 == 0:
                 nc.vector.tensor_copy(out=dst, in_=src)
             else:
                 nc.scalar.copy(out=dst, in_=src)
-            nc.vector.quantize_mx(out=o_codes[:, c0:c1].bitcast(FP8X4), scales=o_scales[:, c0:c1], in_=o_grouped[:, c0 * T : c1 * T])
+            nc.vector.quantize_mx(out=o_codes[:, c0:c1].bitcast(FP8X4), scales=o_scales[:, c0:c1], in_=o_grouped[:, 0 : (c1 - c0) * T])
         nc.sync.dma_start(out=out_1[0].rearrange("p m t -> p (m t)").bitcast(I32), in_=o_codes[:].bitcast(I32))
         for g in range(4):
-            nc.sync.dma_start(out=out_2[0, 4 * g : 4 * g + 4, :].bitcast(I32), in_=o_scales[32 * g : 32 * g + 4, :].bitcast(I32))
+            queue = nc.sync if g % 2 == 0 else nc.scalar
+            queue.dma_start(out=out_2[0, 4 * g : 4 * g + 4, :].bitcast(I32), in_=o_scales[32 * g : 32 * g + 4, :].bitcast(I32))

@@ -21,6 +21,7 @@ P = 128
 T = 4
 BLK = 512
 NB = 4
+SCALAR_TAKES = (1, 0, 0)
 ON_SCALAR = [[1,0,1,1],[1,0,1,1],[1,0,1,1],[1,0,1,1]]
 UNITS = T * K
 AHEAD = 5
@@ -34,8 +35,7 @@ def tile_bigramconvkernelpoolingmatch_x1_kernel(tc, q, x, w, bias, gain, mu, sig
         work = ctx.enter_context(tc.tile_pool(name="work", bufs=2))
         ypool = ctx.enter_context(tc.tile_pool(name="ypool", bufs=9))
         spsum = ctx.enter_context(tc.psum_pool(name="spsum", bufs=4))
-        xpsum = ctx.enter_context(tc.psum_pool(name="xpsum", bufs=2))
-        upsum = ctx.enter_context(tc.psum_pool(name="upsum", bufs=2))
+        upsum = ctx.enter_context(tc.psum_pool(name="upsum", bufs=4))
 
         gain_sb = keep.tile([P, 4], BF16, name="gain_sb")
         bias_sb = keep.tile([P, 4], BF16, name="bias_sb")
@@ -167,10 +167,7 @@ def tile_bigramconvkernelpoolingmatch_x1_kernel(tc, q, x, w, bias, gain, mu, sig
 
         def convolve(j):
             for t in range(T):
-                if t < 2:
-                    h_bank = xpsum.tile([P, BLK], F32, name="h_bank", tag="xb")
-                else:
-                    h_bank = upsum.tile([P, BLK], F32, name="h_bank", tag="u")
+                h_bank = upsum.tile([P, BLK], F32, name="h_bank", tag="u")
                 h_banks[j, t] = h_bank
             for s in range(2):
                 cols = slice(j * BLK + s * P, j * BLK + s * P + BLK)
@@ -258,23 +255,32 @@ def tile_bigramconvkernelpoolingmatch_x1_kernel(tc, q, x, w, bias, gain, mu, sig
             nc.vector.tensor_tensor(out=m[:], in0=source[:, 0:width], in1=source[:, width : 2 * width], op=ALU.min)
             part[u] = m[:]
 
-        def subtract(u, h):
-            y = y_tiles[u][:, h * 1024 : (h + 1) * 1024].rearrange("p (n i) -> p n i", n=8)
-            nc.vector.tensor_tensor(out=y, in0=y, in1=r_tiles[u][:].unsqueeze(1).to_broadcast([P, 8, P]), op=ALU.subtract)
+        def subtract(u, first, last):
+            y = y_tiles[u][:, first * BLK : last * BLK].rearrange("p (n i) -> p n i", i=P)
+            nearest_square = r_tiles[u][:].unsqueeze(1).to_broadcast([P, (last - first) * NB, P])
+            nc.vector.tensor_tensor(out=y, in0=y, in1=nearest_square, op=ALU.subtract)
 
         def exponent(u, first, last):
             y = y_tiles[u][:, first * BLK : last * BLK]
             nc.scalar.activation(out=y, in_=y, func=ACT.Exp, scale=-1.0)
 
-        sum_banks = {}
+        rows = [keep.tile([P, B, 2 * K], F32, name="rows%d" % t) for t in range(T)]
+        row_banks = {}
+
+        def place(t, slot):
+            return row_banks[t, slot // 4][:, slot % 4, :]
 
         def add_up(u, j):
+            t, k = divmod(u, K)
+            if k == 0 and j == 0:
+                for c in range(3):
+                    row_bank = upsum.tile([P, 4, P], F32, name="row_bank", tag="u")
+                    row_banks[t, c] = row_bank
             if j == 0:
-                sum_banks[u] = upsum.tile([P, 2, P], F32, name="sum_bank", tag="u")
-                nc.tensor.transpose(sum_banks[u][:, 1, :], r_tiles[u][:], ident[:])
+                nc.tensor.transpose(place(t, K + k), r_tiles[u][:], ident[:])
             for n in range(j * NB, (j + 1) * NB):
                 nc.tensor.matmul(
-                    sum_banks[u][:, 0, :],
+                    place(t, k),
                     lhsT=y_tiles[u][:, n * P : (n + 1) * P],
                     rhs=ident[:],
                     is_transpose=True,
@@ -282,27 +288,13 @@ def tile_bigramconvkernelpoolingmatch_x1_kernel(tc, q, x, w, bias, gain, mu, sig
                     stop=(n == N - 1),
                 )
 
-        stats = {}
-
-        reordered = keep.tile([P, T - 1, 2, B * K], F32, name="reordered")
-
-        def take_sum(u):
-            t, k = divmod(u, K)
-            if k == 0:
-                stats[t] = work.tile([P, 2, K, B], F32, name="stats", tag="st")
-            if u % 2 == 1 and u < UNITS - 2:
-                nc.scalar.copy(out=stats[t][:, :, k, :], in_=sum_banks[u][:])
+        def take(t, c):
+            out = rows[t][:, :, 4 * c : 4 * c + 4]
+            in_ = row_banks[t, c][:].rearrange("p c b -> p b c")
+            if SCALAR_TAKES[c] and t < T - 1:
+                nc.scalar.copy(out=out, in_=in_)
             else:
-                nc.vector.tensor_copy(out=stats[t][:, :, k, :], in_=sum_banks[u][:])
-            if k == K - 1 and t < T - 1:
-                nc.gpsimd.tensor_scalar(
-                    out=reordered[:, t].rearrange("p s (b k) -> p s b k", k=K),
-                    in0=stats[t][:].rearrange("p s k b -> p s b k"),
-                    scalar1=1.0,
-                    scalar2=0.0,
-                    op0=ALU.mult,
-                    op1=ALU.add,
-                )
+                nc.vector.tensor_copy(out=out, in_=in_)
 
         gain_neg = keep.tile([P, 4], F32, name="gain_neg")
         gain_abs = keep.tile([P, 4], F32, name="gain_abs")
@@ -417,26 +409,32 @@ def tile_bigramconvkernelpoolingmatch_x1_kernel(tc, q, x, w, bias, gain, mu, sig
                     score(u // K, j)
                 square(u, j)
 
-        for step in range(4):
+        for step in range(3):
             nearest(0, step)
             nearest(1, step)
-        subtract(0, 0)
-        subtract(0, 1)
+        nearest(0, 3)
+        subtract(0, 0, 4)
         for u in range(UNITS):
             if u + 2 < UNITS:
                 nearest(u + 2, 0)
             if u + 1 < UNITS:
-                subtract(u + 1, 0)
+                nearest(u + 1, 3)
             if u + 2 < UNITS:
                 nearest(u + 2, 1)
             if u + 1 < UNITS:
-                subtract(u + 1, 1)
+                if u + 1 < UNITS - 1:
+                    subtract(u + 1, 0, 4)
+                else:
+                    for j in range(4):
+                        subtract(u + 1, j, j + 1)
             if u + 2 < UNITS:
                 nearest(u + 2, 2)
-            if u >= 2:
-                take_sum(u - 2)
-            if u + 2 < UNITS:
-                nearest(u + 2, 3)
+            t, k = divmod(u, K)
+            if k == 5:
+                take(t, 0)
+            if k == 1 and t > 0:
+                take(t - 1, 2)
+                take(t - 1, 1)
             if 1 <= u < UNITS - 1:
                 for j in range(4):
                     add_up(u - 1, j)
@@ -448,25 +446,21 @@ def tile_bigramconvkernelpoolingmatch_x1_kernel(tc, q, x, w, bias, gain, mu, sig
                     add_up(u, j)
             for i in range(4):
                 next_square()
-        take_sum(UNITS - 2)
-        take_sum(UNITS - 1)
+        take(T - 1, 2)
 
         res = keep.tile([P, T, B * K], F32, name="res")
-        last = stats[T - 1]
-        for t in range(T - 1):
-            nc.scalar.activation(out=reordered[:, t, 0, :], in_=reordered[:, t, 0, :], func=ACT.Ln, scale=1.0 / N)
-        nc.scalar.activation(out=last[:, 0, 0 : K - 1], in_=last[:, 0, 0 : K - 1], func=ACT.Ln, scale=1.0 / N)
-        nc.scalar.activation(out=last[:, 0, K - 1], in_=last[:, 0, K - 1], func=ACT.Ln, scale=1.0 / N)
         for t in range(T):
-            if t < T - 1:
-                nc.vector.tensor_tensor(out=res[:, t, :], in0=reordered[:, t, 0], in1=reordered[:, t, 1], op=ALU.subtract)
-            else:
-                nc.vector.tensor_tensor(
-                    out=res[:, t, :].rearrange("p (b k) -> p b k", k=K),
-                    in0=last[:, 0].rearrange("p k b -> p b k"),
-                    in1=last[:, 1].rearrange("p k b -> p b k"),
-                    op=ALU.subtract,
-                )
+            if t == T - 2:
+                take(T - 1, 1)
+            nc.scalar.activation(
+                out=res[:, t, :].rearrange("p (b k) -> p b k", k=K), in_=rows[t][:, :, 0:K], func=ACT.Ln, scale=1.0 / N
+            )
+            nc.vector.tensor_tensor(
+                out=res[:, t, :].rearrange("p (b k) -> p b k", k=K),
+                in0=res[:, t, :].rearrange("p (b k) -> p b k", k=K),
+                in1=rows[t][:, :, K : 2 * K],
+                op=ALU.subtract,
+            )
             nc.sync.dma_start(out=out_0.rearrange("(p t) b k -> p t (b k)", t=T)[:, t, :], in_=res[:, t, :])
         o_codes = keep.tile([P, B * K], U32, align_bytes=64, name="o_codes")
         o_scales = keep.tile([P, B * K], U8, align_bytes=64, name="o_scales")

from contextlib import ExitStack

import concourse.mybir as mybir
from concourse.masks import make_identity

Q, B, N, D, E, K = 512, 128, 16, 512, 512, 6
FLOPS = 2 * (2 * B * N * D * E + Q * B * N * E)

F32 = mybir.dt.float32
BF16 = mybir.dt.bfloat16
U32 = mybir.dt.uint32
I32 = mybir.dt.int32
U8 = mybir.dt.uint8
FP8X4 = mybir.dt.float8_e4m3fn_x4
ACT = mybir.ActivationFunctionType
ALU = mybir.AluOpType
AX = mybir.AxisListType
ENG = mybir.EngineType

P = 128
T = 4
BLK = 512
NB = 4
SCALAR_TAKES = (1, 0, 0)
ON_SCALAR = [[1,0,1,1],[1,0,1,1],[1,0,1,1],[1,0,1,1]]
UNITS = T * K
AHEAD = 5


def tile_bigramconvkernelpoolingmatch_x1_kernel(tc, q, x, w, bias, gain, mu, sigma, out_0, out_1, out_2):
    nc = tc.nc
    with ExitStack() as ctx:
        ctx.enter_context(tc.manual_schedule())
        keep = ctx.enter_context(tc.tile_pool(name="keep", bufs=1))
        work = ctx.enter_context(tc.tile_pool(name="work", bufs=2))
        ypool = ctx.enter_context(tc.tile_pool(name="ypool", bufs=9))
        spsum = ctx.enter_context(tc.psum_pool(name="spsum", bufs=4))
        upsum = ctx.enter_context(tc.psum_pool(name="upsum", bufs=4))

        gain_sb = keep.tile([P, 4], BF16, name="gain_sb")
        bias_sb = keep.tile([P, 4], BF16, name="bias_sb")
        mu_sb = keep.tile([P, K], BF16, name="mu_sb")
        sigma_sb = keep.tile([P, K], BF16, name="sigma_sb")
        nc.scalar.dma_start(out=gain_sb[:], in_=gain.rearrange("(p t) -> p t", t=4))
        nc.scalar.dma_start(out=bias_sb[:], in_=bias.rearrange("(p t) -> p t", t=4))
        nc.scalar.dma_start(out=mu_sb[:], in_=mu.partition_broadcast(P))
        nc.scalar.dma_start(out=sigma_sb[:], in_=sigma.partition_broadcast(P))

        x_groups = [(0, 1), (1, 5), (5, 9), (9, 13), (13, 17)]
        x_raw = {}

        def load_x(g):
            n0, n1 = x_groups[g]
            x_raw[g] = work.tile([P, (n1 - n0) * D], BF16, name="x_raw", tag="x0" if g == 0 else "xr", bufs=1 if g == 0 else 3)
            nc.sync.dma_start(out=x_raw[g][:], in_=x[:, n0:n1, :].rearrange("b n d -> b (n d)"))

        w_raw = []
        for s in range(2):
            w_raw.append(keep.tile([P, 4, E], BF16, name="w_raw%d" % s))
        q_raw = keep.tile([P, T * E], BF16, name="q_raw")

        def load_w(s):
            nc.sync.dma_start(out=w_raw[s][:], in_=w[s].rearrange("(p j) c -> p j c", j=4))

        def load_q():
            nc.sync.dma_start(out=q_raw[:], in_=q.rearrange("(m t) k -> m (t k)", t=T))

        load_x(0)
        load_x(1)
        load_w(0)
        load_x(2)
        load_w(1)
        load_x(3)
        load_q()

        ident = keep.tile([P, P], F32, name="ident")
        make_identity(nc, ident[:])

        w_codes = []
        w_scales = []
        for s in range(2):
            w_codes.append(keep.tile([P, E], U32, align_bytes=64, name="w_codes%d" % s))
            w_scales.append(keep.tile([P, E], U8, align_bytes=64, name="w_scales%d" % s))
        x_codes = keep.tile([P, (N + 1) * B], U32, align_bytes=64, name="x_codes")
        x_scales = keep.tile([P, (N + 1) * B], U8, align_bytes=64, name="x_scales")
        q_codes = keep.tile([P, Q], U32, align_bytes=64, name="q_codes")
        q_scales = keep.tile([P, Q], U8, align_bytes=64, name="q_scales")
        d_codes = keep.tile([P, N * B], U32, align_bytes=64, name="d_codes")
        d_scales = keep.tile([P, N * B], U8, align_bytes=64, name="d_scales")

        def transpose_words(raw, slot, bank, place):
            words = raw[:, slot * D : (slot + 1) * D].bitcast(F32)
            for u in range(2):
                nc.tensor.transpose(bank[:, place, u, :], words[:, u : D // 2 : 2], ident[:])

        turn_banks = {}

        def turn_pair(raw, first, n, key):
            bank = spsum.tile([P, 2, 2, P], F32, name="x_bank", tag="s")
            for place in range(n):
                transpose_words(raw, first + place, bank, place)
            turn_banks[key] = bank

        def copy_pair(grouped, first, n, key):
            cols = slice(first * P * 4, (first + n) * P * 4)
            nc.scalar.copy(
                out=grouped[:, cols].bitcast(F32).rearrange("p (n r u) -> p n r u", n=n, u=2),
                in_=turn_banks[key][:, 0:n].rearrange("p n u r -> p n r u"),
            )

        w_grouped = {}

        def interleave_w(s):
            w_grouped[s] = work.tile([P, 4 * E], BF16, align_bytes=64, name="w_grouped", tag="wg")
            nc.vector.tensor_copy(
                out=w_grouped[s][:].rearrange("p (t m j) -> p t m j", t=4, j=4),
                in_=w_raw[s][:].rearrange("p j (m t) -> p t m j", t=4),
            )

        def quantise_w(s):
            nc.vector.quantize_mx(out=w_codes[s][:].bitcast(FP8X4), scales=w_scales[s][:], in_=w_grouped[s][:])

        x_grouped = {}

        def turn_x(g, s):
            n0, n1 = x_groups[g]
            turn_pair(x_raw[g], s, min(2, n1 - n0 - s), ("x", g, s))

        def copy_x(g, s):
            n0, n1 = x_groups[g]
            if s == 0:
                x_grouped[g] = work.tile([P, 4 * 4 * P], BF16, align_bytes=64, name="x_grouped", tag="xg")
            copy_pair(x_grouped[g], s, min(2, n1 - n0 - s), ("x", g, s))

        def quantise_x(g):
            n0, n1 = x_groups[g]
            cols = slice(n0 * P, n1 * P)
            nc.vector.quantize_mx(
                out=x_codes[:, cols].bitcast(FP8X4), scales=x_scales[:, cols], in_=x_grouped[g][:, 0 : (n1 - n0) * P * 4]
            )

        q_tiles = {}

        def turn_q(s):
            turn_pair(q_raw, s, 2, ("q", s))

        def copy_q(s):
            if s == 0:
                q_tiles["grouped"] = work.tile([P, 4 * Q], BF16, align_bytes=64, name="q_grouped", tag="qg", bufs=1)
            copy_pair(q_tiles["grouped"], s, 2, ("q", s))

        def sign_q():
            q_tiles["signed"] = work.tile([P, 4 * Q], BF16, align_bytes=64, name="q_signed", tag="wg")
            nc.vector.tensor_tensor(
                out=q_tiles["signed"][:].rearrange("p (c j) -> p c j", j=4),
                in0=q_tiles["grouped"][:].rearrange("p (c j) -> p c j", j=4),
                in1=sign[:].unsqueeze(1).to_broadcast([P, Q, 4]),
                op=ALU.mult,
            )

        def quantise_q():
            nc.vector.quantize_mx(out=q_codes[:].bitcast(FP8X4), scales=q_scales[:], in_=q_tiles["signed"][:])

        d_sep = {}

        h_banks = {}

        def convolve(j):
            for t in range(T):
                h_bank = upsum.tile([P, BLK], F32, name="h_bank", tag="u")
                h_banks[j, t] = h_bank
            for s in range(2):
                cols = slice(j * BLK + s * P, j * BLK + s * P + BLK)
                for t in range(T):
                    nc.tensor.matmul_mx(
                        out=h_banks[j, t][:],
                        lhsT=w_codes[s][:, t * P : (t + 1) * P].bitcast(FP8X4),
                        lhsT_scale=w_scales[s][:, t * P : (t + 1) * P],
                        rhs=x_codes[:, cols].bitcast(FP8X4),
                        rhs_scale=x_scales[:, cols],
                        start=(s == 0),
                        stop=(s == 1),
                    )

        def rectify(j, t):
            if t == 0:
                d_sep[j] = work.tile([P, T, BLK], BF16, name="d_sep", tag="ds")
            if ON_SCALAR[j][t]:
                nc.scalar.activation(
                    out=d_sep[j][:, t, :], in_=h_banks[j, t][:], func=ACT.Identity, bias=gain_bias[:, t : t + 1], scale=gain_abs[:, t : t + 1]
                )
            else:
                nc.vector.tensor_scalar(
                    out=d_sep[j][:, t, :], in0=h_banks[j, t][:], scalar1=gain_abs[:, t : t + 1], scalar2=gain_bias[:, t : t + 1], op0=ALU.mult, op1=ALU.add
                )

        d_grouped = {}

        def interleave_d(j):
            d_grouped[j] = work.tile([P, 4 * BLK], BF16, align_bytes=64, name="d_grouped", tag="dg")
            nc.vector.tensor_scalar(
                out=d_grouped[j][:].rearrange("p (c t) -> p c t", t=T),
                in0=d_sep[j][:].rearrange("p t c -> p c t"),
                scalar1=0.0,
                scalar2=None,
                op0=ALU.max,
            )

        def quantise_d(j):
            cols = slice(j * BLK, (j + 1) * BLK)
            nc.vector.quantize_mx(out=d_codes[:, cols].bitcast(FP8X4), scales=d_scales[:, cols], in_=d_grouped[j][:])

        score_banks = {}

        def score(t, j):
            bank = spsum.tile([P, BLK], F32, name="s_bank", tag="s")
            for i in range(NB):
                cols = slice((j * NB + i) * B, (j * NB + i + 1) * B)
                nc.tensor.matmul_mx(
                    out=bank[:, i * P : (i + 1) * P],
                    lhsT=d_codes[:, cols].bitcast(FP8X4),
                    lhsT_scale=d_scales[:, cols],
                    rhs=q_codes[:, t * P : (t + 1) * P].bitcast(FP8X4),
                    rhs_scale=q_scales[:, t * P : (t + 1) * P],
                    start=True,
                    stop=True,
                )
            score_banks[j] = bank

        y_tiles = {}

        def square(u, j):
            k = u % K
            if j == 0:
                y_tiles[u] = ypool.tile([P, N * P], F32, name="y", tag="y")
            nc.scalar.activation(
                out=y_tiles[u][:, j * BLK : (j + 1) * BLK],
                in_=score_banks[j][:],
                func=ACT.Square,
                bias=z_bias[:, k : k + 1],
                scale=z_scale[:, k : k + 1],
            )

        r_tiles = {}
        part = {}

        def nearest(u, step):
            width = 1024 >> step
            source = y_tiles[u][:] if step == 0 else part[u]
            if step < 3:
                m = work.tile([P, width], F32, name="m%d" % step, tag="m%d" % step)
            else:
                m = work.tile([P, width], F32, name="r", tag="r", bufs=4)
                r_tiles[u] = m
            nc.vector.tensor_tensor(out=m[:], in0=source[:, 0:width], in1=source[:, width : 2 * width], op=ALU.min)
            part[u] = m[:]

        def subtract(u, first, last):
            y = y_tiles[u][:, first * BLK : last * BLK].rearrange("p (n i) -> p n i", i=P)
            nearest_square = r_tiles[u][:].unsqueeze(1).to_broadcast([P, (last - first) * NB, P])
            nc.vector.tensor_tensor(out=y, in0=y, in1=nearest_square, op=ALU.subtract)

        def exponent(u, first, last):
            y = y_tiles[u][:, first * BLK : last * BLK]
            nc.scalar.activation(out=y, in_=y, func=ACT.Exp, scale=-1.0)

        rows = [keep.tile([P, B, 2 * K], F32, name="rows%d" % t) for t in range(T)]
        row_banks = {}

        def place(t, slot):
            return row_banks[t, slot // 4][:, slot % 4, :]

        def add_up(u, j):
            t, k = divmod(u, K)
            if k == 0 and j == 0:
                for c in range(3):
                    row_bank = upsum.tile([P, 4, P], F32, name="row_bank", tag="u")
                    row_banks[t, c] = row_bank
            if j == 0:
                nc.tensor.transpose(place(t, K + k), r_tiles[u][:], ident[:])
            for n in range(j * NB, (j + 1) * NB):
                nc.tensor.matmul(
                    place(t, k),
                    lhsT=y_tiles[u][:, n * P : (n + 1) * P],
                    rhs=ident[:],
                    is_transpose=True,
                    start=(n == 0),
                    stop=(n == N - 1),
                )

        def take(t, c):
            out = rows[t][:, :, 4 * c : 4 * c + 4]
            in_ = row_banks[t, c][:].rearrange("p c b -> p b c")
            if SCALAR_TAKES[c] and t < T - 1:
                nc.scalar.copy(out=out, in_=in_)
            else:
                nc.vector.tensor_copy(out=out, in_=in_)

        gain_neg = keep.tile([P, 4], F32, name="gain_neg")
        gain_abs = keep.tile([P, 4], F32, name="gain_abs")
        gain_bias = keep.tile([P, 4], F32, name="gain_bias")
        sign01 = keep.tile([P, 4], F32, name="sign01")
        sign = keep.tile([P, 4], BF16, name="sign")
        z_scale = keep.tile([P, K], F32, name="z_scale")
        z_bias = keep.tile([P, K], F32, name="z_bias")
        rsig = keep.tile([P, K], F32, name="rsig")
        nc.vector.tensor_scalar(out=gain_neg[:], in0=gain_sb[:], scalar1=-1.0, scalar2=None, op0=ALU.mult)
        nc.vector.reciprocal(out=rsig[:], in_=sigma_sb[:])
        nc.vector.tensor_tensor(out=gain_abs[:], in0=gain_sb[:], in1=gain_neg[:], op=ALU.max)
        nc.vector.tensor_scalar(out=z_scale[:], in0=rsig[:], scalar1=0.7071067811865476, scalar2=None, op0=ALU.mult)
        nc.vector.tensor_tensor(out=gain_bias[:], in0=gain_abs[:], in1=bias_sb[:], op=ALU.mult)
        nc.vector.scalar_tensor_tensor(out=z_bias[:], in0=mu_sb[:], scalar=-1.0, in1=z_scale[:], op0=ALU.mult, op1=ALU.mult)
        nc.vector.tensor_scalar(out=sign01[:], in0=gain_sb[:], scalar1=0.0, scalar2=2.0, op0=ALU.is_ge, op1=ALU.mult)
        nc.vector.tensor_scalar(out=sign[:], in0=sign01[:], scalar1=1.0, scalar2=None, op0=ALU.subtract)

        turn_x(0, 0)
        copy_x(0, 0)
        turn_x(1, 0)
        turn_x(1, 2)
        copy_x(1, 0)
        copy_x(1, 2)
        interleave_w(0)
        quantise_x(0)
        quantise_x(1)
        quantise_w(0)
        turn_x(2, 0)
        turn_x(2, 2)
        copy_x(2, 0)
        copy_x(2, 2)
        interleave_w(1)
        quantise_w(1)
        quantise_x(2)
        load_x(4)
        turn_x(3, 0)
        turn_x(3, 2)
        copy_x(3, 0)
        copy_x(3, 2)
        convolve(0)
        rectify(0, 0)
        rectify(0, 1)
        rectify(0, 2)
        rectify(0, 3)
        turn_q(0)
        turn_q(2)
        copy_q(0)
        copy_q(2)
        interleave_d(0)
        quantise_x(3)
        quantise_d(0)
        convolve(1)
        rectify(1, 0)
        rectify(1, 1)
        rectify(1, 2)
        rectify(1, 3)
        turn_x(4, 0)
        turn_x(4, 2)
        copy_x(4, 0)
        copy_x(4, 2)
        sign_q()
        interleave_d(1)
        quantise_x(4)
        quantise_d(1)
        convolve(2)
        rectify(2, 0)
        rectify(2, 1)
        rectify(2, 2)
        rectify(2, 3)
        quantise_q()
        score(0, 0)
        square(0, 0)
        square(1, 0)
        interleave_d(2)
        quantise_d(2)
        convolve(3)
        score(0, 1)
        rectify(3, 0)
        rectify(3, 1)
        rectify(3, 2)
        rectify(3, 3)
        square(0, 1)
        square(1, 1)
        score(0, 2)
        square(0, 2)
        interleave_d(3)
        quantise_d(3)
        score(0, 3)
        square(1, 2)
        square(0, 3)
        square(1, 3)
        square(2, 0)
        square(2, 1)
        square(2, 2)
        square(2, 3)
        square(3, 0)
        square(3, 1)
        square(3, 2)
        square(3, 3)
        square(4, 0)
        square(4, 1)
        square(4, 2)
        square(4, 3)

        squares = [(u, j) for u in range(AHEAD, UNITS) for j in range(4)]

        def next_square():
            if squares:
                u, j = squares.pop(0)
                if u % K == 0:
                    score(u // K, j)
                square(u, j)

        for step in range(3):
            nearest(0, step)
            nearest(1, step)
        nearest(0, 3)
        subtract(0, 0, 4)
        for u in range(UNITS):
            if u + 2 < UNITS:
                nearest(u + 2, 0)
            if u + 1 < UNITS:
                nearest(u + 1, 3)
            if u + 2 < UNITS:
                nearest(u + 2, 1)
            if u + 1 < UNITS:
                if u + 1 < UNITS - 1:
                    subtract(u + 1, 0, 4)
                else:
                    for j in range(4):
                        subtract(u + 1, j, j + 1)
            if u + 2 < UNITS:
                nearest(u + 2, 2)
            t, k = divmod(u, K)
            if k == 5:
                take(t, 0)
            if k == 1 and t > 0:
                take(t - 1, 2)
                take(t - 1, 1)
            if 1 <= u < UNITS - 1:
                for j in range(4):
                    add_up(u - 1, j)
            if u < UNITS - 2:
                exponent(u, 0, 4)
            else:
                for j in range(4):
                    exponent(u, j, j + 1)
                    add_up(u, j)
            for i in range(4):
                next_square()
        take(T - 1, 2)

        res = keep.tile([P, T, B * K], F32, name="res")
        for t in range(T):
            if t == T - 2:
                take(T - 1, 1)
            nc.scalar.activation(
                out=res[:, t, :].rearrange("p (b k) -> p b k", k=K), in_=rows[t][:, :, 0:K], func=ACT.Ln, scale=1.0 / N
            )
            nc.vector.tensor_tensor(
                out=res[:, t, :].rearrange("p (b k) -> p b k", k=K),
                in0=res[:, t, :].rearrange("p (b k) -> p b k", k=K),
                in1=rows[t][:, :, K : 2 * K],
                op=ALU.subtract,
            )
            nc.sync.dma_start(out=out_0.rearrange("(p t) b k -> p t (b k)", t=T)[:, t, :], in_=res[:, t, :])
        o_codes = keep.tile([P, B * K], U32, align_bytes=64, name="o_codes")
        o_scales = keep.tile([P, B * K], U8, align_bytes=64, name="o_scales")
        for c0, c1 in ((0, 512), (512, 768)):
            o_grouped = work.tile([P, 4 * BLK], BF16, align_bytes=64, name="o_grouped", tag="dg")
            src = res[:, :, c0:c1].rearrange("p t c -> p c t")
            dst = o_grouped[:, 0 : (c1 - c0) * T].rearrange("p (c t) -> p c t", t=T)
            if c0 == 0:
                nc.vector.tensor_copy(out=dst, in_=src)
            else:
                nc.scalar.copy(out=dst, in_=src)
            nc.vector.quantize_mx(out=o_codes[:, c0:c1].bitcast(FP8X4), scales=o_scales[:, c0:c1], in_=o_grouped[:, 0 : (c1 - c0) * T])
        nc.sync.dma_start(out=out_1[0].rearrange("p m t -> p (m t)").bitcast(I32), in_=o_codes[:].bitcast(I32))
        for g in range(4):
            queue = nc.sync if g % 2 == 0 else nc.scalar
            queue.dma_start(out=out_2[0, 4 * g : 4 * g + 4, :].bitcast(I32), in_=o_scales[32 * g : 32 * g + 4, :].bitcast(I32))
